import numpy as np
import ml_dtypes


def mxq(x, axis, fmt="e4m3"):
    dtype, down = {"e4m3": (ml_dtypes.float8_e4m3fn, 7), "e5m2": (ml_dtypes.float8_e5m2, 14)}[fmt]
    v = np.moveaxis(np.asarray(x, np.float32).astype(ml_dtypes.bfloat16).astype(np.float64), axis, -1)
    blocks = v.reshape(v.shape[:-1] + (-1, 32))
    amax = np.abs(blocks).max(-1, keepdims=True)
    byte = np.maximum(np.where(amax > 0, np.frexp(amax)[1] - 1 + 127, 0) - down, 1)
    scale = np.exp2(byte - 127.0)
    codes = (blocks / scale).astype(np.float32).astype(dtype).astype(np.float64)
    return np.moveaxis((codes * scale).reshape(v.shape), -1, axis)


WIDE = False


def mx_kscale(k):
    if not WIDE:
        return np.ones(k)
    levels = np.array([10, -10, 5, -5, 0])
    if k % 512:
        return np.exp2(np.random.permutation(np.resize(levels, k // 32))).repeat(32)
    a = np.empty((k // 512, 16))
    for p in range(k // 512):
        a[p, :8] = np.random.permutation(np.resize(levels, 8))
        for g in range(8):
            far = levels[np.abs(levels - a[p, g]) >= 10]
            a[p, g + 8] = far[np.random.randint(len(far))]
    return np.exp2(a.ravel()).repeat(32)


def f64(x):
    return np.asarray(x).astype(np.float64)


def striped(idx):
    return np.tile(idx.reshape(-1, 16).T, (8, 1)).astype(np.uint16)


def unstriped(offs):
    return offs[:16].T.reshape(-1).astype(np.int64)


E2M1 = np.array([0.0, 0.5, 1.0, 1.5, 2.0, 3.0, 4.0, 6.0, -0.0, -0.5, -1.0, -1.5, -2.0, -3.0, -4.0, -6.0])


def pack_weight(w, fmt):
    k, n = w.shape
    w = f64(np.asarray(w, np.float32).astype(ml_dtypes.bfloat16)).reshape(k // 32, 32, n)
    amax = np.abs(w).max(1)
    if fmt == "e4m3":
        byte = np.frexp(amax)[1] - 1 + 127 - 7
    else:
        mant, ex = np.frexp(amax / 6.0)
        byte = np.where(mant > 0.5, ex, ex - 1) + 127
    byte = np.clip(np.where(amax > 0, byte, 1), 1, 254)
    scaled = (w * np.exp2(127.0 - byte)[:, None, :]).reshape(k, n).astype(np.float32)
    by_word = np.ascontiguousarray(scaled.reshape(k // 512, 128, 4, n).transpose(0, 1, 3, 2))
    if fmt == "e4m3":
        words = by_word.astype(ml_dtypes.float8_e4m3fn).view(np.uint8)
    else:
        c = by_word.astype(ml_dtypes.float4_e2m1fn).view(np.uint8) & 0xF
        words = (c[..., 0::2] | (c[..., 1::2] << 4)).reshape(k // 512, 128, 2 * n)
    return np.ascontiguousarray(words), np.ascontiguousarray(byte.astype(np.uint8).reshape(k // 512, 16, n))


def unpack_weight(words, scales, fmt):
    g, _, n = scales.shape
    words = np.ascontiguousarray(words).reshape(g, 128, n, -1)
    if fmt == "e4m3":
        vals = words.view(ml_dtypes.float8_e4m3fn).astype(np.float64)
    else:
        nib = np.empty((g, 128, n, 4), np.uint8)
        nib[..., 0::2] = words & 0xF
        nib[..., 1::2] = words >> 4
        vals = E2M1[nib]
    vals = vals * np.repeat(np.exp2(scales.astype(np.float64) - 127.0), 8, axis=1)[..., None]
    return vals.transpose(0, 1, 3, 2).reshape(g * 512, n)


def silu(v):
    return v / (1.0 + np.exp(-np.maximum(v, -700.0)))


K, T, E, C, N = 512, 1536, 8, 256, 256
PAD = 32


def by_expert(wq, xq):
    return np.concatenate([wq[e].T @ xq[:, e * C:(e + 1) * C] for e in range(E)], axis=1)


def setup_inputs():
    n = np.random.standard_normal
    s = mx_kscale(K)[:, None]
    first = np.random.permutation(np.repeat(np.arange(E), T // E))
    second = (first + 1 + np.random.permutation(np.repeat(np.arange(E - 1), -(-T // (E - 1)))[:T])) % E
    while np.bincount(second, minlength=E).max() != T // E:
        load = np.bincount(second, minlength=E); hi, lo = int(load.argmax()), int(load.argmin())
        t = np.flatnonzero((second == hi) & (first != lo))[0]; second[t] = lo
    slot_token = np.empty(E * C, np.int64); pos = np.empty((2, T), np.int64); fill = np.zeros(E, np.int64)
    place = np.stack([np.random.permutation(C) for _ in range(E)])
    for r, deal in enumerate((first, second)):
        for t in np.random.permutation(T):
            e = deal[t]
            if fill[e] < C: j = e * C + place[e, fill[e]]; fill[e] += 1; slot_token[j] = t; pos[r, t] = j
            else: pos[r, t] = E * C + t % PAD
    g = np.random.uniform(0.2, 0.8, T)
    w = [pack_weight(m, "e2m1") for m in n((E, K, N)) / np.sqrt(K) / s[None]]
    return {
        "xT": (n((K, T)) * s).astype(np.float32),
        "w_words": np.stack([m[0] for m in w]),
        "w_scales": np.stack([m[1] for m in w]),
        "b": (0.3 * n((N, E))).astype(np.float32),
        "gate": np.stack([np.tile(g, (N, 1)), np.tile(1.0 - g, (N, 1))]).astype(np.float32),
        "offs": striped(slot_token),
        "pos1": striped(pos[0]),
        "pos2": striped(pos[1]),
    }


def reference(xT, w_words, w_scales, b, gate, offs, pos1, pos2):
    idx = unstriped(offs)
    w = np.stack([unpack_weight(w_words[e], w_scales[e], "e2m1") for e in range(E)])
    xq = mxq(f64(xT)[:, idx], 0, "e4m3")
    y = by_expert(w, xq)
    y = silu(y + np.repeat(f64(b), C, axis=1))
    y = np.concatenate([y, np.zeros((N, PAD))], axis=1)
    return f64(gate[0]) * y[:, unstriped(pos1)] + f64(gate[1]) * y[:, unstriped(pos2)]

@@ -1,0 +1,127 @@
+import concourse.mybir as mybir
+
+K, T, E, C, N = 512, 1536, 8, 256, 256
+PAD = 32
+P = 128
+SLOTS = E * C
+HALVES = N // P
+
+F32 = mybir.dt.float32
+BF16 = mybir.dt.bfloat16
+I32 = mybir.dt.int32
+U32 = mybir.dt.uint32
+U16 = mybir.dt.uint16
+U8 = mybir.dt.uint8
+FP8X4 = mybir.dt.float8_e4m3fn_x4
+FP4X4 = mybir.dt.float4_e2m1fn_x4
+COPY = mybir.ActivationFunctionType.Copy
+SILU = mybir.ActivationFunctionType.Silu
+MULT = mybir.AluOpType.mult
+ADD = mybir.AluOpType.add
+
+FLOPS = 2 * SLOTS * K * N
+BYTES = 4 * (K * T + N * T + 2 * T + N * E) + E * (K * N // 2 + 16 * N) + 2 * (SLOTS + 2 * T)
+
+CHUNKS = ((0, 512, 192), (512, 512, 192), (1024, 256, 96), (1280, 256, 96))
+GATHERS = ((0, 512), (512, 512), (1024, 512), (1536, 256), (1792, 256))
+PIECES = ((0, 0, 512), (0, 512, 512), (0, 1024, 512), (1, 0, 512), (1, 512, 512), (1, 1024, 256), (1, 1280, 256))
+
+
+def tile_moe_cap2_lin_silu_kernel(tc, xT, w_words, w_scales, b, gate, offs, pos1, pos2, out):
+    nc = tc.nc
+    with (
+        tc.tile_pool(name="lists", bufs=1) as lists,
+        tc.tile_pool(name="keep", bufs=1) as keep,
+        tc.psum_pool(name="psum", bufs=8) as psum,
+    ):
+        offs_sb = lists.tile([P, SLOTS // 16], U16, name="offs_sb")
+        pos1_sb = lists.tile([P, T // 16], U16, name="pos1_sb")
+        pos2_sb = lists.tile([P, T // 16], U16, name="pos2_sb")
+
+        words = keep.tile([P, T], U32, name="words", align_bytes=64)
+        scales = keep.tile([P, T], U8, name="scales", align_bytes=64)
+        slot_words = keep.tile([P, SLOTS], U32, name="slot_words", align_bytes=64)
+        slot_scales = keep.tile([P, SLOTS], U8, name="slot_scales", align_bytes=64)
+        w_sb = keep.tile([P, E, 2 * N], U8, name="w_sb", align_bytes=64)
+        ws_sb = keep.tile([P, E, N], U8, name="ws_sb", align_bytes=64)
+        b_sb = keep.tile([P, HALVES, E], F32, name="b_sb")
+        gates = [keep.tile([P, T], F32, name=f"gate{c}") for c in range(2)]
+        y = [keep.tile([P, SLOTS + PAD], F32, name=f"y{h}") for h in range(HALVES)]
+        warm = keep.tile([P, 1], F32, name="warm")
+
+        x_rows = xT.rearrange("(p j) t -> p j t", j=4)
+        raws = []
+        for i, (t0, tw, s) in enumerate(CHUNKS):
+            raw = keep.tile([P, 4, tw], F32, name=f"raw{i}")
+            nc.sync.dma_start(raw[:], x_rows[:, :, t0 : t0 + tw])
+            raws.append(raw)
+        nc.sync.dma_start(offs_sb[:], offs)
+
+        nc.vector.memset(warm[:], 0.0)
+        nc.scalar.activation(warm[:], warm[:], SILU)
+        nc.gpsimd.memset(scales[:], 0)
+        nc.gpsimd.memset(ws_sb[:], 0)
+        for h in range(HALVES):
+            nc.gpsimd.memset(y[h][:, SLOTS:], 0.0)
+
+        ws_rows = w_scales.bitcast(I32)
+        for q in range(4):
+            nc.sync.dma_start(
+                ws_sb[32 * q : 32 * q + 4].bitcast(I32),
+                ws_rows[:, 0, 4 * q : 4 * q + 4, :].rearrange("e q n -> q e n"),
+            )
+        nc.sync.dma_start(w_sb[:].bitcast(I32), w_words.bitcast(I32).rearrange("e a p c -> p (e a) c"))
+        nc.sync.dma_start(b_sb[:], b.rearrange("(h p) e -> p h e", h=HALVES))
+        nc.sync.dma_start(pos1_sb[:], pos1)
+        nc.sync.dma_start(pos2_sb[:], pos2)
+        for c in range(2):
+            nc.sync.dma_start(gates[c][:], gate[c, 0:P, :])
+
+        for i, (t0, tw, s) in enumerate(CHUNKS):
+            v = tw - s
+            xb = keep.tile([P, tw, 4], BF16, name=f"xb{i}", align_bytes=64)
+            nc.scalar.activation(xb[:, v:, :], raws[i][:, :, v:].rearrange("p j w -> p w j"), COPY)
+            nc.vector.tensor_copy(xb[:, :v, :], raws[i][:, :, :v].rearrange("p j w -> p w j"))
+            nc.vector.quantize_mx(
+                out=words[:, t0 : t0 + tw].bitcast(FP8X4),
+                scales=scales[:, t0 : t0 + tw],
+                in_=xb[:].rearrange("p w j -> p (w j)"),
+            )
+
+        for s0, sw in GATHERS:
+            some = offs_sb[:, s0 // 16 : (s0 + sw) // 16]
+            nc.vector.tensor_copy(slot_words[:, s0 : s0 + sw], words[:].indirect(some))
+            nc.vector.tensor_copy(slot_scales[:, s0 : s0 + sw], scales[:].indirect(some))
+            for e in range(s0 // C, (s0 + sw) // C):
+                cols = slice(e * C, (e + 1) * C)
+                for h in range(HALVES):
+                    acc = psum.tile([P, 512], F32, name="acc")
+                    nc.tensor.matmul_mx(
+                        out=acc[:, :C],
+                        lhsT=w_sb[:, e, 2 * P * h : 2 * P * (h + 1)].bitcast(FP4X4),
+                        lhsT_scale=ws_sb[:, e, P * h : P * (h + 1)],
+                        rhs=slot_words[:, cols].bitcast(FP8X4),
+                        rhs_scale=slot_scales[:, cols],
+                        start=True,
+                        stop=True,
+                    )
+                    nc.scalar.activation(y[h][:, cols], acc[:, :C], SILU, bias=b_sb[:, h, e : e + 1])
+
+        waiting = None
+        for i, (h, t0, tw) in enumerate(PIECES):
+            toks = slice(t0, t0 + tw)
+            place = slice(t0 // 16, (t0 + tw) // 16)
+            first = keep.tile([P, tw], F32, name=f"first{i}")
+            second = keep.tile([P, tw], F32, name=f"second{i}")
+            nc.vector.tensor_tensor(first[:], y[h][:].indirect(pos1_sb[:, place]), gates[0][:, toks], MULT)
+            nc.vector.tensor_tensor(second[:], y[h][:].indirect(pos2_sb[:, place]), gates[1][:, toks], MULT)
+            if waiting is not None:
+                finish(nc, keep, out, *waiting)
+            waiting = (i, h, toks, first, second)
+        finish(nc, keep, out, *waiting)
+
+
+def finish(nc, keep, out, i, h, toks, first, second):
+    both = keep.tile([P, toks.stop - toks.start], F32, name=f"both{i}")
+    nc.vector.tensor_tensor(both[:], first[:], second[:], ADD)
+    nc.sync.dma_start(out[h * P : (h + 1) * P, toks], both[:])

@@ -22,9 +22,10 @@ ADD = mybir.AluOpType.add
 FLOPS = 2 * SLOTS * K * N
 BYTES = 4 * (K * T + N * T + 2 * T + N * E) + E * (K * N // 2 + 16 * N) + 2 * (SLOTS + 2 * T)
 
-CHUNKS = ((0, 512, 192), (512, 512, 192), (1024, 256, 96), (1280, 256, 96))
+LOADS = ((0, 768), (768, 512), (1280, 256))
+CHUNKS = ((0, 512, 192), (512, 256, 96), (768, 512, 192), (1280, 256, 96))
 GATHERS = ((0, 512), (512, 512), (1024, 512), (1536, 256), (1792, 256))
-PIECES = ((0, 0, 512), (0, 512, 512), (0, 1024, 512), (1, 0, 512), (1, 512, 512), (1, 1024, 256), (1, 1280, 256))
+LAST = ((0, 768), (768, 512), (1280, 128), (1408, 128))
 
 
 def tile_moe_cap2_lin_silu_kernel(tc, xT, w_words, w_scales, b, gate, offs, pos1, pos2, out):
@@ -50,11 +51,12 @@ def tile_moe_cap2_lin_silu_kernel(tc, xT, w_words, w_scales, b, gate, offs, pos1
         warm = keep.tile([P, 1], F32, name="warm")
 
         x_rows = xT.rearrange("(p j) t -> p j t", j=4)
-        raws = []
-        for i, (t0, tw, s) in enumerate(CHUNKS):
+        raws = {}
+        for i, (t0, tw) in enumerate(LOADS):
             raw = keep.tile([P, 4, tw], F32, name=f"raw{i}")
             nc.sync.dma_start(raw[:], x_rows[:, :, t0 : t0 + tw])
-            raws.append(raw)
+            for t in range(t0, t0 + tw, 64):
+                raws[t] = raw, t - t0
         nc.sync.dma_start(offs_sb[:], offs)
 
         nc.vector.memset(warm[:], 0.0)
@@ -79,9 +81,10 @@ def tile_moe_cap2_lin_silu_kernel(tc, xT, w_words, w_scales, b, gate, offs, pos1
 
         for i, (t0, tw, s) in enumerate(CHUNKS):
             v = tw - s
+            raw, r0 = raws[t0]
             xb = keep.tile([P, tw, 4], BF16, name=f"xb{i}", align_bytes=64)
-            nc.scalar.activation(xb[:, v:, :], raws[i][:, :, v:].rearrange("p j w -> p w j"), COPY)
-            nc.vector.tensor_copy(xb[:, :v, :], raws[i][:, :, :v].rearrange("p j w -> p w j"))
+            nc.scalar.activation(xb[:, v:, :], raw[:, :, r0 + v : r0 + tw].rearrange("p j w -> p w j"), COPY)
+            nc.vector.tensor_copy(xb[:, :v, :], raw[:, :, r0 : r0 + v].rearrange("p j w -> p w j"))
             nc.vector.quantize_mx(
                 out=words[:, t0 : t0 + tw].bitcast(FP8X4),
                 scales=scales[:, t0 : t0 + tw],
@@ -107,21 +110,27 @@ def tile_moe_cap2_lin_silu_kernel(tc, xT, w_words, w_scales, b, gate, offs, pos1
                     )
                     nc.scalar.activation(y[h][:, cols], acc[:, :C], SILU, bias=b_sb[:, h, e : e + 1])
 
-        waiting = None
-        for i, (h, t0, tw) in enumerate(PIECES):
+        first = [keep.tile([P, T], F32, name=f"first{h}") for h in range(HALVES)]
+        second = [keep.tile([P, T], F32, name=f"second{h}") for h in range(HALVES)]
+        both = [keep.tile([P, T], F32, name=f"both{h}") for h in range(HALVES)]
+
+        def product(dest, h, pos, c, t0, tw):
+            place = pos[:] if tw == T else pos[:, t0 // 16 : (t0 + tw) // 16]
+            nc.vector.tensor_tensor(dest[h][:, t0 : t0 + tw], y[h][:].indirect(place), gates[c][:, t0 : t0 + tw], MULT)
+
+        def finish(h, t0, tw):
             toks = slice(t0, t0 + tw)
-            place = slice(t0 // 16, (t0 + tw) // 16)
-            first = keep.tile([P, tw], F32, name=f"first{i}")
-            second = keep.tile([P, tw], F32, name=f"second{i}")
-            nc.vector.tensor_tensor(first[:], y[h][:].indirect(pos1_sb[:, place]), gates[0][:, toks], MULT)
-            nc.vector.tensor_tensor(second[:], y[h][:].indirect(pos2_sb[:, place]), gates[1][:, toks], MULT)
-            if waiting is not None:
-                finish(nc, keep, out, *waiting)
-            waiting = (i, h, toks, first, second)
-        finish(nc, keep, out, *waiting)
+            nc.vector.tensor_tensor(both[h][:, toks], first[h][:, toks], second[h][:, toks], ADD)
+            nc.sync.dma_start(out[h * P : (h + 1) * P, toks], both[h][:, toks])
 
-
-def finish(nc, keep, out, i, h, toks, first, second):
-    both = keep.tile([P, toks.stop - toks.start], F32, name=f"both{i}")
-    nc.vector.tensor_tensor(both[:], first[:], second[:], ADD)
-    nc.sync.dma_start(out[h * P : (h + 1) * P, toks], both[:])
+        product(first, 0, pos1_sb, 0, 0, T)
+        product(second, 0, pos2_sb, 1, 0, T)
+        product(first, 1, pos1_sb, 0, 0, T)
+        finish(0, 0, T)
+        before = None
+        for t0, tw in LAST:
+            product(second, 1, pos2_sb, 1, t0, tw)
+            if before is not None:
+                finish(1, *before)
+            before = (t0, tw)
+        finish(1, *before)

@@ -23,8 +23,8 @@ FLOPS = 2 * SLOTS * K * N
 BYTES = 4 * (K * T + N * T + 2 * T + N * E) + E * (K * N // 2 + 16 * N) + 2 * (SLOTS + 2 * T)
 
 LOADS = ((0, 768), (768, 512), (1280, 256))
-CHUNKS = ((0, 512, 192), (512, 256, 96), (768, 512, 192), (1280, 256, 96))
-GATHERS = ((0, 512), (512, 512), (1024, 512), (1536, 256), (1792, 256))
+CHUNKS = ((0, 512, 256), (512, 256, 128), (768, 512, 256), (1280, 256, 96))
+GATHERS = ((0, 512, 512), (512, 512, 512), (1024, 512, 512), (1536, 512, 256))
 LAST = ((0, 768), (768, 512), (1280, 128), (1408, 128))
 
 
@@ -91,24 +91,27 @@ def tile_moe_cap2_lin_silu_kernel(tc, xT, w_words, w_scales, b, gate, offs, pos1
                 in_=xb[:].rearrange("p w j -> p (w j)"),
             )
 
-        for s0, sw in GATHERS:
-            some = offs_sb[:, s0 // 16 : (s0 + sw) // 16]
-            nc.vector.tensor_copy(slot_words[:, s0 : s0 + sw], words[:].indirect(some))
-            nc.vector.tensor_copy(slot_scales[:, s0 : s0 + sw], scales[:].indirect(some))
-            for e in range(s0 // C, (s0 + sw) // C):
-                cols = slice(e * C, (e + 1) * C)
-                for h in range(HALVES):
-                    acc = psum.tile([P, 512], F32, name="acc")
-                    nc.tensor.matmul_mx(
-                        out=acc[:, :C],
-                        lhsT=w_sb[:, e, 2 * P * h : 2 * P * (h + 1)].bitcast(FP4X4),
-                        lhsT_scale=ws_sb[:, e, P * h : P * (h + 1)],
-                        rhs=slot_words[:, cols].bitcast(FP8X4),
-                        rhs_scale=slot_scales[:, cols],
-                        start=True,
-                        stop=True,
-                    )
-                    nc.scalar.activation(y[h][:, cols], acc[:, :C], SILU, bias=b_sb[:, h, e : e + 1])
+        def expert(e, h):
+            cols = slice(e * C, (e + 1) * C)
+            acc = psum.tile([P, 512], F32, name="acc")
+            nc.tensor.matmul_mx(
+                out=acc[:, :C],
+                lhsT=w_sb[:, e, 2 * P * h : 2 * P * (h + 1)].bitcast(FP4X4),
+                lhsT_scale=ws_sb[:, e, P * h : P * (h + 1)],
+                rhs=slot_words[:, cols].bitcast(FP8X4),
+                rhs_scale=slot_scales[:, cols],
+                start=True,
+                stop=True,
+            )
+            nc.scalar.activation(y[h][:, cols], acc[:, :C], SILU, bias=b_sb[:, h, e : e + 1])
+
+        for s0, sw, bw in GATHERS:
+            nc.vector.tensor_copy(slot_words[:, s0 : s0 + sw], words[:].indirect(offs_sb[:, s0 // 16 : (s0 + sw) // 16]))
+            for b0 in range(s0, s0 + sw, bw):
+                nc.vector.tensor_copy(slot_scales[:, b0 : b0 + bw], scales[:].indirect(offs_sb[:, b0 // 16 : (b0 + bw) // 16]))
+                for e in range(b0 // C, (b0 + bw) // C):
+                    for h in range(HALVES):
+                        expert(e, h)
 
         first = [keep.tile([P, T], F32, name=f"first{h}") for h in range(HALVES)]
         second = [keep.tile([P, T], F32, name=f"second{h}") for h in range(HALVES)]

import concourse.mybir as mybir

K, T, E, C, N = 512, 1536, 8, 256, 256
PAD = 32
P = 128
SLOTS = E * C
HALVES = N // P

F32 = mybir.dt.float32
BF16 = mybir.dt.bfloat16
I32 = mybir.dt.int32
U32 = mybir.dt.uint32
U16 = mybir.dt.uint16
U8 = mybir.dt.uint8
FP8X4 = mybir.dt.float8_e4m3fn_x4
FP4X4 = mybir.dt.float4_e2m1fn_x4
COPY = mybir.ActivationFunctionType.Copy
SILU = mybir.ActivationFunctionType.Silu
MULT = mybir.AluOpType.mult
ADD = mybir.AluOpType.add

FLOPS = 2 * SLOTS * K * N
BYTES = 4 * (K * T + N * T + 2 * T + N * E) + E * (K * N // 2 + 16 * N) + 2 * (SLOTS + 2 * T)

LOADS = ((0, 768), (768, 512), (1280, 256))
CHUNKS = ((0, 512, 256), (512, 256, 128), (768, 512, 256), (1280, 256, 96))
GATHERS = ((0, 512, 512), (512, 512, 512), (1024, 512, 512), (1536, 512, 256))
LAST = ((0, 768), (768, 512), (1280, 128), (1408, 128))


def tile_moe_cap2_lin_silu_kernel(tc, xT, w_words, w_scales, b, gate, offs, pos1, pos2, out):
    nc = tc.nc
    with (
        tc.tile_pool(name="lists", bufs=1) as lists,
        tc.tile_pool(name="keep", bufs=1) as keep,
        tc.psum_pool(name="psum", bufs=8) as psum,
    ):
        offs_sb = lists.tile([P, SLOTS // 16], U16, name="offs_sb")
        pos1_sb = lists.tile([P, T // 16], U16, name="pos1_sb")
        pos2_sb = lists.tile([P, T // 16], U16, name="pos2_sb")

        words = keep.tile([P, T], U32, name="words", align_bytes=64)
        scales = keep.tile([P, T], U8, name="scales", align_bytes=64)
        slot_words = keep.tile([P, SLOTS], U32, name="slot_words", align_bytes=64)
        slot_scales = keep.tile([P, SLOTS], U8, name="slot_scales", align_bytes=64)
        w_sb = keep.tile([P, E, 2 * N], U8, name="w_sb", align_bytes=64)
        ws_sb = keep.tile([P, E, N], U8, name="ws_sb", align_bytes=64)
        b_sb = keep.tile([P, HALVES, E], F32, name="b_sb")
        gates = [keep.tile([P, T], F32, name=f"gate{c}") for c in range(2)]
        y = [keep.tile([P, SLOTS + PAD], F32, name=f"y{h}") for h in range(HALVES)]
        warm = keep.tile([P, 1], F32, name="warm")

        x_rows = xT.rearrange("(p j) t -> p j t", j=4)
        raws = {}
        for i, (t0, tw) in enumerate(LOADS):
            raw = keep.tile([P, 4, tw], F32, name=f"raw{i}")
            nc.sync.dma_start(raw[:], x_rows[:, :, t0 : t0 + tw])
            for t in range(t0, t0 + tw, 64):
                raws[t] = raw, t - t0
        nc.sync.dma_start(offs_sb[:], offs)

        nc.vector.memset(warm[:], 0.0)
        nc.scalar.activation(warm[:], warm[:], SILU)
        nc.gpsimd.memset(scales[:], 0)
        nc.gpsimd.memset(ws_sb[:], 0)
        for h in range(HALVES):
            nc.gpsimd.memset(y[h][:, SLOTS:], 0.0)

        ws_rows = w_scales.bitcast(I32)
        for q in range(4):
            nc.sync.dma_start(
                ws_sb[32 * q : 32 * q + 4].bitcast(I32),
                ws_rows[:, 0, 4 * q : 4 * q + 4, :].rearrange("e q n -> q e n"),
            )
        nc.sync.dma_start(w_sb[:].bitcast(I32), w_words.bitcast(I32).rearrange("e a p c -> p (e a) c"))
        nc.sync.dma_start(b_sb[:], b.rearrange("(h p) e -> p h e", h=HALVES))
        nc.sync.dma_start(pos1_sb[:], pos1)
        nc.sync.dma_start(pos2_sb[:], pos2)
        for c in range(2):
            nc.sync.dma_start(gates[c][:], gate[c, 0:P, :])

        for i, (t0, tw, s) in enumerate(CHUNKS):
            v = tw - s
            raw, r0 = raws[t0]
            xb = keep.tile([P, tw, 4], BF16, name=f"xb{i}", align_bytes=64)
            nc.scalar.activation(xb[:, v:, :], raw[:, :, r0 + v : r0 + tw].rearrange("p j w -> p w j"), COPY)
            nc.vector.tensor_copy(xb[:, :v, :], raw[:, :, r0 : r0 + v].rearrange("p j w -> p w j"))
            nc.vector.quantize_mx(
                out=words[:, t0 : t0 + tw].bitcast(FP8X4),
                scales=scales[:, t0 : t0 + tw],
                in_=xb[:].rearrange("p w j -> p (w j)"),
            )

        def expert(e, h):
            cols = slice(e * C, (e + 1) * C)
            acc = psum.tile([P, 512], F32, name="acc")
            nc.tensor.matmul_mx(
                out=acc[:, :C],
                lhsT=w_sb[:, e, 2 * P * h : 2 * P * (h + 1)].bitcast(FP4X4),
                lhsT_scale=ws_sb[:, e, P * h : P * (h + 1)],
                rhs=slot_words[:, cols].bitcast(FP8X4),
                rhs_scale=slot_scales[:, cols],
                start=True,
                stop=True,
            )
            nc.scalar.activation(y[h][:, cols], acc[:, :C], SILU, bias=b_sb[:, h, e : e + 1])

        for s0, sw, bw in GATHERS:
            nc.vector.tensor_copy(slot_words[:, s0 : s0 + sw], words[:].indirect(offs_sb[:, s0 // 16 : (s0 + sw) // 16]))
            for b0 in range(s0, s0 + sw, bw):
                nc.vector.tensor_copy(slot_scales[:, b0 : b0 + bw], scales[:].indirect(offs_sb[:, b0 // 16 : (b0 + bw) // 16]))
                for e in range(b0 // C, (b0 + bw) // C):
                    for h in range(HALVES):
                        expert(e, h)

        first = [keep.tile([P, T], F32, name=f"first{h}") for h in range(HALVES)]
        second = [keep.tile([P, T], F32, name=f"second{h}") for h in range(HALVES)]
        both = [keep.tile([P, T], F32, name=f"both{h}") for h in range(HALVES)]

        def product(dest, h, pos, c, t0, tw):
            place = pos[:] if tw == T else pos[:, t0 // 16 : (t0 + tw) // 16]
            nc.vector.tensor_tensor(dest[h][:, t0 : t0 + tw], y[h][:].indirect(place), gates[c][:, t0 : t0 + tw], MULT)

        def finish(h, t0, tw):
            toks = slice(t0, t0 + tw)
            nc.vector.tensor_tensor(both[h][:, toks], first[h][:, toks], second[h][:, toks], ADD)
            nc.sync.dma_start(out[h * P : (h + 1) * P, toks], both[h][:, toks])

        product(first, 0, pos1_sb, 0, 0, T)
        product(second, 0, pos2_sb, 1, 0, T)
        product(first, 1, pos1_sb, 0, 0, T)
        finish(0, 0, T)
        before = None
        for t0, tw in LAST:
            product(second, 1, pos2_sb, 1, t0, tw)
            if before is not None:
                finish(1, *before)
            before = (t0, tw)
        finish(1, *before)
